import numpy as np
import ml_dtypes


def mxq(x, axis, fmt="e4m3"):
    dtype, down = {"e4m3": (ml_dtypes.float8_e4m3fn, 7), "e5m2": (ml_dtypes.float8_e5m2, 14)}[fmt]
    v = np.moveaxis(np.asarray(x, np.float32).astype(ml_dtypes.bfloat16).astype(np.float64), axis, -1)
    blocks = v.reshape(v.shape[:-1] + (-1, 32))
    amax = np.abs(blocks).max(-1, keepdims=True)
    byte = np.maximum(np.where(amax > 0, np.frexp(amax)[1] - 1 + 127, 0) - down, 1)
    scale = np.exp2(byte - 127.0)
    codes = (blocks / scale).astype(np.float32).astype(dtype).astype(np.float64)
    return np.moveaxis((codes * scale).reshape(v.shape), -1, axis)


WIDE = False


def mx_kscale(k):
    if not WIDE:
        return np.ones(k)
    levels = np.array([30, -30])
    if k % 512:
        return np.exp2(np.random.permutation(np.resize(levels, k // 32))).repeat(32)
    a = np.empty((k // 512, 16))
    for p in range(k // 512):
        a[p, :8] = np.random.permutation(np.resize(levels, 8))
        for g in range(8):
            far = levels[np.abs(levels - a[p, g]) >= 10]
            a[p, g + 8] = far[np.random.randint(len(far))]
    return np.exp2(a.ravel()).repeat(32)


def f64(x):
    return np.asarray(x).astype(np.float64)


def striped(idx):
    return np.tile(np.asarray(idx).reshape(-1, 16).T, (8, 1)).astype(np.uint16)


def unstriped(offs):
    return offs[:16].T.reshape(-1).astype(np.int64)


E2M1 = np.array([0.0, 0.5, 1.0, 1.5, 2.0, 3.0, 4.0, 6.0, -0.0, -0.5, -1.0, -1.5, -2.0, -3.0, -4.0, -6.0])


def pack_weight(w, fmt):
    k, n = w.shape
    w = f64(np.asarray(w, np.float32).astype(ml_dtypes.bfloat16)).reshape(k // 32, 32, n)
    amax = np.abs(w).max(1)
    if fmt in ("e4m3", "e5m2"):
        byte = np.frexp(amax)[1] - 1 + 127 - (7 if fmt == "e4m3" else 14)
    else:
        mant, ex = np.frexp(amax / 6.0)
        byte = np.where(mant > 0.5, ex, ex - 1) + 127
    byte = np.clip(np.where(amax > 0, byte, 1), 1, 254)
    scaled = (w * np.exp2(127.0 - byte)[:, None, :]).reshape(k, n).astype(np.float32)
    by_word = np.ascontiguousarray(scaled.reshape(k // 512, 128, 4, n).transpose(0, 1, 3, 2))
    if fmt in ("e4m3", "e5m2"):
        words = by_word.astype(ml_dtypes.float8_e4m3fn if fmt == "e4m3" else ml_dtypes.float8_e5m2).view(np.uint8)
    else:
        c = by_word.astype(ml_dtypes.float4_e2m1fn).view(np.uint8) & 0xF
        words = (c[..., 0::2] | (c[..., 1::2] << 4)).reshape(k // 512, 128, 2 * n)
    return np.ascontiguousarray(words), np.ascontiguousarray(byte.astype(np.uint8).reshape(k // 512, 16, n))


def unpack_weight(words, scales, fmt):
    g, _, n = scales.shape
    words = np.ascontiguousarray(words).reshape(g, 128, n, -1)
    if fmt in ("e4m3", "e5m2"):
        vals = words.view(ml_dtypes.float8_e4m3fn if fmt == "e4m3" else ml_dtypes.float8_e5m2).astype(np.float64)
    else:
        nib = np.empty((g, 128, n, 4), np.uint8)
        nib[..., 0::2] = words & 0xF
        nib[..., 1::2] = words >> 4
        vals = E2M1[nib]
    vals = vals * np.repeat(np.exp2(scales.astype(np.float64) - 127.0), 8, axis=1)[..., None]
    return vals.transpose(0, 1, 3, 2).reshape(g * 512, n)


K, T, J, R, C, O, N, E = 512, 1024, 256, 512, 512, 256, 256, 128


def setup_inputs():
    n = np.random.standard_normal
    idx = np.random.permutation(T)[:J]
    idx2 = np.random.permutation(C)[:J]
    idx3 = np.random.permutation(C)[:J]
    idx4 = np.random.permutation(C)[:O]
    idx5 = np.random.permutation(O)[:E]
    idx6 = np.random.permutation(O)[:E]
    fk = mx_kscale(K)
    fr = mx_kscale(R)
    xtp = pack_weight(n((K, T)) / fk[:, None], "e2m1")
    wp = pack_weight(n((K, R)) * 1 / np.sqrt(K) * fk[:, None] * fr, "e4m3")
    w2p = pack_weight(n((K, R)) * 1 / np.sqrt(K) * fk[:, None] * fr, "e5m2")
    wbp = pack_weight(n((R, N)) * 1 / np.sqrt(R) / fr[:, None], "e2m1")
    return {
        "xt_words": xtp[0],
        "xt_scales": xtp[1],
        "w_words": wp[0],
        "w_scales": wp[1],
        "w2_words": w2p[0],
        "w2_scales": w2p[1],
        "wb_words": wbp[0],
        "wb_scales": wbp[1],
        "offs": striped(idx),
        "offs2": striped(idx2),
        "offs3": striped(idx3),
        "offs4": striped(idx4),
        "offs5": striped(idx5),
        "offs6": striped(idx6),
    }


def reference(xt_words, xt_scales, w_words, w_scales, w2_words, w2_scales, wb_words, wb_scales, offs, offs2, offs3, offs4, offs5, offs6):
    idx = unstriped(offs)
    idx2 = unstriped(offs2)
    idx3 = unstriped(offs3)
    idx4 = unstriped(offs4)
    idx5 = unstriped(offs5)
    idx6 = unstriped(offs6)
    xtu = unpack_weight(xt_words, xt_scales, "e2m1")
    wu = unpack_weight(w_words, w_scales, "e4m3")
    w2u = unpack_weight(w2_words, w2_scales, "e5m2")
    wbu = unpack_weight(wb_words, wb_scales, "e2m1")
    xtidxg = xtu[:, idx]
    a = wu.T @ xtidxg
    b = w2u.T @ xtidxg
    pw = np.zeros((R, C))
    pw[:, idx2] = a
    pv = np.zeros((R, C))
    pv[:, idx3] = b
    pg = pw + pv
    hid = pg[:, idx4]
    hidq = mxq(hid, 0, "e5m2")
    p = wbu.T @ hidq
    y = np.maximum(p[:, idx5], p[:, idx6])
    return y

@@ -1,0 +1,192 @@
+from contextlib import ExitStack
+
+import concourse.mybir as mybir
+
+K, T, J, R, C, O, N, E = 512, 1024, 256, 512, 512, 256, 256, 128
+FLOPS = 2 * K * R * J * 2 + 2 * R * N * O
+
+F32 = mybir.dt.float32
+BF16 = mybir.dt.bfloat16
+I32 = mybir.dt.int32
+U32 = mybir.dt.uint32
+U16 = mybir.dt.uint16
+U8 = mybir.dt.uint8
+E4M3 = mybir.dt.float8_e4m3fn_x4
+E5M2 = mybir.dt.float8_e5m2_x4
+E2M1 = mybir.dt.float4_e2m1fn_x4
+COPY = mybir.ActivationFunctionType.Copy
+ADD = mybir.AluOpType.add
+MAX = mybir.AluOpType.max
+
+P = 128
+PACK = 4
+
+
+def load_scale_rows(queue, plane, scales):
+    for q in range(4):
+        queue.dma_start(out=plane[32 * q : 32 * q + 4, :].bitcast(I32), in_=scales[0, 4 * q : 4 * q + 4, :].bitcast(I32))
+
+
+def tile_list_twow_shared_one_bestoftwo_kernel(
+    tc, xt_words, xt_scales, w_words, w_scales, w2_words, w2_scales, wb_words, wb_scales,
+    offs, offs2, offs3, offs4, offs5, offs6, out,
+):
+    nc = tc.nc
+    with ExitStack() as ctx:
+        sb = ctx.enter_context(tc.tile_pool(name="sb", bufs=1))
+        psum = ctx.enter_context(tc.psum_pool(name="psum", bufs=8))
+
+        lists = [sb.tile([P, src.shape[1]], U16, name="list%d" % i) for i, src in enumerate((offs, offs2, offs3, offs4, offs5, offs6))]
+        l_tok, l_a, l_b, l_read, l_p1, l_p2 = lists
+
+        x_words = sb.tile([P, T], U16, tag="x_then_pv1", align_bytes=64)
+        x_plane = sb.tile([P, T], U8, align_bytes=64)
+        w_raw = [sb.tile([P, R], U32, name="w_raw%d" % i, tag="w_then_pv%d" % (2 * i), align_bytes=64) for i in range(2)]
+        ws_raw = [sb.tile([P, R], U8, name="ws_raw%d" % i, align_bytes=64) for i in range(2)]
+        wb_codes = sb.tile([P, 2 * N], U8, align_bytes=64)
+        wb_plane = sb.tile([P, N], U8, align_bytes=64)
+
+        nc.vector.memset(x_plane[:].bitcast(I32), 0)
+        nc.vector.memset(ws_raw[0][:].bitcast(I32), 0)
+        nc.gpsimd.memset(ws_raw[1][:].bitcast(I32), 0)
+        nc.gpsimd.memset(wb_plane[:].bitcast(I32), 0)
+
+        nc.sync.dma_start(out=x_words[:].bitcast(I32), in_=xt_words[0].bitcast(I32))
+        nc.sync.dma_start(l_tok[:], offs)
+        load_scale_rows(nc.sync, x_plane, xt_scales)
+        nc.sync.dma_start(out=w_raw[0][:].bitcast(I32), in_=w_words[0].rearrange("p n t -> p (n t)").bitcast(I32))
+        load_scale_rows(nc.sync, ws_raw[0], w_scales)
+        nc.sync.dma_start(out=w_raw[1][:].bitcast(I32), in_=w2_words[0].rearrange("p n t -> p (n t)").bitcast(I32))
+        nc.sync.dma_start(l_a[:], offs2)
+        load_scale_rows(nc.sync, ws_raw[1], w2_scales)
+        nc.sync.dma_start(l_b[:], offs3)
+        nc.sync.dma_start(l_read[:], offs4)
+        nc.sync.dma_start(out=wb_codes[:].bitcast(I32), in_=wb_words[0].bitcast(I32))
+        load_scale_rows(nc.sync, wb_plane, wb_scales)
+        nc.sync.dma_start(l_p1[:], offs5)
+        nc.sync.dma_start(l_p2[:], offs6)
+
+        pw = [sb.tile([P, C], F32, name="pw%d" % t) for t in range(PACK)]
+        for b in pw:
+            nc.vector.memset(b[:], 0.0)
+
+        xg_words = sb.tile([P, J], U16, align_bytes=64)
+        xg_plane = sb.tile([P, J], U8, align_bytes=64)
+        nc.vector.tensor_copy(xg_words[:], x_words[:].indirect(l_tok[:]))
+        nc.vector.tensor_copy(xg_plane[:], x_plane[:].indirect(l_tok[:]))
+
+        w_codes = [sb.tile([P, R], U32, name="w_codes%d" % i, align_bytes=64) for i in range(2)]
+        w_plane = [sb.tile([P, R], U8, name="w_plane%d" % i, align_bytes=64) for i in range(2)]
+
+        def deal_words(m):
+            nc.scalar.copy(
+                out=w_codes[m][:].rearrange("p (t c i) -> p c t i", t=PACK, i=4),
+                in_=w_raw[m][:].rearrange("p (c i t) -> p c t i", t=PACK, i=4),
+            )
+
+        def deal_scales(m, engine):
+            engine.tensor_copy(
+                out=w_plane[m][:].rearrange("p (t q) -> p t q", t=PACK),
+                in_=ws_raw[m][:].rearrange("p (q t) -> p t q", t=PACK),
+            )
+
+        deal_words(0)
+        deal_scales(0, nc.vector)
+        deal_words(1)
+        deal_scales(1, nc.gpsimd)
+
+        pv = [
+            sb.tile([P, C], F32, name="pv0", tag="w_then_pv0", align_bytes=64),
+            sb.tile([P, C], F32, name="pv1", tag="x_then_pv1", align_bytes=64),
+            sb.tile([P, C], F32, name="pv2", tag="w_then_pv2", align_bytes=64),
+        ]
+        for b in (pv[1], pv[0], pv[2]):
+            nc.gpsimd.memset(b[:], 0.0)
+        boards = [pw, [pv[t % 3] for t in range(PACK)]]
+
+        fmt = (E4M3, E5M2)
+        place = (l_a, l_b)
+        acc = {}
+
+        def multiply(m, t):
+            bank = psum.tile([P, J], F32, name="bank")
+            cols = slice(P * t, P * (t + 1))
+            nc.tensor.matmul_mx(
+                out=bank[:], lhsT=w_codes[m][:, cols].bitcast(fmt[m]), lhsT_scale=w_plane[m][:, cols],
+                rhs=xg_words[:].bitcast(E2M1), rhs_scale=xg_plane[:], start=True, stop=True,
+            )
+            acc[m, t] = bank
+
+        vals = {}
+
+        def evacuate(m, t, on_vector):
+            v = sb.tile([P, J], F32, name="vals%d_%d" % (m, t))
+            if on_vector:
+                nc.vector.tensor_copy(out=v[:], in_=acc[m, t][:])
+            else:
+                nc.scalar.copy(out=v[:], in_=acc[m, t][:])
+            vals[m, t] = v
+
+        def scatter(m, t, on_vector):
+            window = boards[m][t][:].indirect(place[m][:])
+            if on_vector:
+                nc.vector.tensor_copy(window, vals[m, t][:])
+            else:
+                nc.scalar.activation(window, vals[m, t][:], COPY)
+
+        hid = sb.tile([P, O, PACK], BF16, align_bytes=64)
+
+        def read_board(t):
+            pg = sb.tile([P, C], F32, name="pg%d" % t)
+            nc.vector.tensor_tensor(out=pg[:], in0=boards[0][t][:], in1=boards[1][t][:], op=ADD)
+            nc.vector.tensor_copy(hid[:, :, t], pg[:].indirect(l_read[:]))
+
+        for t in range(PACK):
+            multiply(0, t)
+        evacuate(0, 0, True)
+        evacuate(0, 1, False)
+        scatter(0, 0, True)
+        evacuate(0, 2, False)
+        evacuate(0, 3, False)
+        scatter(0, 1, False)
+        for t in range(PACK):
+            multiply(1, t)
+        scatter(0, 2, True)
+        scatter(0, 3, False)
+        evacuate(1, 0, True)
+        evacuate(1, 1, False)
+        evacuate(1, 2, False)
+        scatter(1, 0, True)
+        scatter(1, 1, False)
+        evacuate(1, 3, False)
+        read_board(0)
+        scatter(1, 2, False)
+        read_board(1)
+        scatter(1, 3, False)
+        read_board(2)
+        read_board(3)
+
+        hid_codes = sb.tile([P, O], U32, align_bytes=64)
+        hid_plane = sb.tile([P, O], U8, align_bytes=64)
+        nc.vector.quantize_mx(out=hid_codes[:].bitcast(E5M2), scales=hid_plane[:], in_=hid[:].rearrange("p o t -> p (o t)"))
+
+        for h in range(N // P):
+            bank = psum.tile([P, O], F32, name="bank")
+            nc.tensor.matmul_mx(
+                out=bank[:], lhsT=wb_codes[:, 2 * P * h : 2 * P * (h + 1)].bitcast(E2M1), lhsT_scale=wb_plane[:, P * h : P * (h + 1)],
+                rhs=hid_codes[:].bitcast(E5M2), rhs_scale=hid_plane[:], start=True, stop=True,
+            )
+            prod = sb.tile([P, O], F32, name="prod%d" % h)
+            first = sb.tile([P, E], F32, name="first%d" % h)
+            second = sb.tile([P, E], F32, name="second%d" % h)
+            best = sb.tile([P, E], F32, name="best%d" % h)
+            if h == 0:
+                nc.vector.tensor_copy(out=prod[:], in_=bank[:])
+                nc.vector.tensor_copy(first[:], prod[:].indirect(l_p1[:]))
+                nc.vector.tensor_copy(second[:], prod[:].indirect(l_p2[:]))
+            else:
+                nc.scalar.copy(out=prod[:], in_=bank[:])
+                nc.scalar.activation(first[:], prod[:].indirect(l_p1[:]), COPY)
+                nc.scalar.activation(second[:], prod[:].indirect(l_p2[:]), COPY)
+            nc.vector.tensor_tensor(out=best[:], in0=first[:], in1=second[:], op=MAX)
+            nc.sync.dma_start(out=out[P * h : P * (h + 1), :], in_=best[:])

@@ -22,8 +22,8 @@ P = 128
 PACK = 4
 
 
-def load_scale_rows(queue, plane, scales):
-    for q in range(4):
+def load_scale_rows(queue, plane, scales, quadrants):
+    for q in quadrants:
         queue.dma_start(out=plane[32 * q : 32 * q + 4, :].bitcast(I32), in_=scales[0, 4 * q : 4 * q + 4, :].bitcast(I32))
 
 
@@ -34,49 +34,57 @@ def tile_list_twow_shared_one_bestoftwo_kernel(
     nc = tc.nc
     with ExitStack() as ctx:
         sb = ctx.enter_context(tc.tile_pool(name="sb", bufs=1))
-        psum = ctx.enter_context(tc.psum_pool(name="psum", bufs=8))
+        psum = ctx.enter_context(tc.psum_pool(name="psum", bufs=1))
 
         lists = [sb.tile([P, src.shape[1]], U16, name="list%d" % i) for i, src in enumerate((offs, offs2, offs3, offs4, offs5, offs6))]
         l_tok, l_a, l_b, l_read, l_p1, l_p2 = lists
 
-        x_words = sb.tile([P, T], U16, tag="x_then_pv1", align_bytes=64)
+        x_words = sb.tile([P, T], U16, tag="x_words", align_bytes=64)
         x_plane = sb.tile([P, T], U8, align_bytes=64)
-        w_raw = [sb.tile([P, R], U32, name="w_raw%d" % i, tag="w_then_pv%d" % (2 * i), align_bytes=64) for i in range(2)]
-        ws_raw = [sb.tile([P, R], U8, name="ws_raw%d" % i, align_bytes=64) for i in range(2)]
+        w_raw = [sb.tile([P, R], U32, name="w_raw%d" % m, tag="w_raw%d" % m, align_bytes=64) for m in range(2)]
+        ws_raw = [sb.tile([P, R], U8, name="ws_raw%d" % m, tag="ws_raw%d" % m, align_bytes=64) for m in range(2)]
         wb_codes = sb.tile([P, 2 * N], U8, align_bytes=64)
         wb_plane = sb.tile([P, N], U8, align_bytes=64)
 
         nc.vector.memset(x_plane[:].bitcast(I32), 0)
         nc.vector.memset(ws_raw[0][:].bitcast(I32), 0)
         nc.gpsimd.memset(ws_raw[1][:].bitcast(I32), 0)
+        load_scale_rows(nc.gpsimd, ws_raw[1], w2_scales, (3,))
         nc.gpsimd.memset(wb_plane[:].bitcast(I32), 0)
 
-        nc.sync.dma_start(out=x_words[:].bitcast(I32), in_=xt_words[0].bitcast(I32))
         nc.sync.dma_start(l_tok[:], offs)
-        load_scale_rows(nc.sync, x_plane, xt_scales)
+        load_scale_rows(nc.sync, x_plane, xt_scales, (0, 1))
+        nc.sync.dma_start(out=x_words[:].bitcast(I32), in_=xt_words[0].bitcast(I32))
+        load_scale_rows(nc.sync, x_plane, xt_scales, (2, 3))
         nc.sync.dma_start(out=w_raw[0][:].bitcast(I32), in_=w_words[0].rearrange("p n t -> p (n t)").bitcast(I32))
-        load_scale_rows(nc.sync, ws_raw[0], w_scales)
+        load_scale_rows(nc.sync, ws_raw[0], w_scales, range(4))
         nc.sync.dma_start(out=w_raw[1][:].bitcast(I32), in_=w2_words[0].rearrange("p n t -> p (n t)").bitcast(I32))
         nc.sync.dma_start(l_a[:], offs2)
-        load_scale_rows(nc.sync, ws_raw[1], w2_scales)
+        load_scale_rows(nc.sync, ws_raw[1], w2_scales, range(3))
         nc.sync.dma_start(l_b[:], offs3)
         nc.sync.dma_start(l_read[:], offs4)
         nc.sync.dma_start(out=wb_codes[:].bitcast(I32), in_=wb_words[0].bitcast(I32))
-        load_scale_rows(nc.sync, wb_plane, wb_scales)
+        load_scale_rows(nc.sync, wb_plane, wb_scales, range(4))
         nc.sync.dma_start(l_p1[:], offs5)
         nc.sync.dma_start(l_p2[:], offs6)
 
-        pw = [sb.tile([P, C], F32, name="pw%d" % t) for t in range(PACK)]
-        for b in pw:
-            nc.vector.memset(b[:], 0.0)
+        boards = {}
+
+        def clear_board(m, t, engine, tag):
+            boards[m, t] = sb.tile([P, C], F32, name="board%d_%d" % (m, t), tag=tag, align_bytes=64)
+            engine.memset(boards[m, t][:], 0.0)
+
+        for m in range(2):
+            for t in range(2):
+                clear_board(m, t, nc.vector, "board%d_%d" % (m, t))
 
         xg_words = sb.tile([P, J], U16, align_bytes=64)
         xg_plane = sb.tile([P, J], U8, align_bytes=64)
         nc.vector.tensor_copy(xg_words[:], x_words[:].indirect(l_tok[:]))
         nc.vector.tensor_copy(xg_plane[:], x_plane[:].indirect(l_tok[:]))
 
-        w_codes = [sb.tile([P, R], U32, name="w_codes%d" % i, align_bytes=64) for i in range(2)]
-        w_plane = [sb.tile([P, R], U8, name="w_plane%d" % i, align_bytes=64) for i in range(2)]
+        w_codes = [sb.tile([P, R], U32, name="w_codes%d" % m, align_bytes=64) for m in range(2)]
+        w_plane = [sb.tile([P, R], U8, name="w_plane%d" % m, align_bytes=64) for m in range(2)]
 
         def deal_words(m):
             nc.scalar.copy(
@@ -84,109 +92,125 @@ def tile_list_twow_shared_one_bestoftwo_kernel(
                 in_=w_raw[m][:].rearrange("p (c i t) -> p c t i", t=PACK, i=4),
             )
 
-        def deal_scales(m, engine):
+        def deal_scales(m, engine, t0, t1):
             engine.tensor_copy(
-                out=w_plane[m][:].rearrange("p (t q) -> p t q", t=PACK),
-                in_=ws_raw[m][:].rearrange("p (q t) -> p t q", t=PACK),
+                out=w_plane[m][:].rearrange("p (t q) -> p t q", t=PACK)[:, t0:t1, :],
+                in_=ws_raw[m][:].rearrange("p (q t) -> p t q", t=PACK)[:, t0:t1, :],
             )
 
         deal_words(0)
-        deal_scales(0, nc.vector)
+        deal_scales(0, nc.vector, 0, 2)
+        deal_scales(0, nc.vector, 2, PACK)
         deal_words(1)
-        deal_scales(1, nc.gpsimd)
-
-        pv = [
-            sb.tile([P, C], F32, name="pv0", tag="w_then_pv0", align_bytes=64),
-            sb.tile([P, C], F32, name="pv1", tag="x_then_pv1", align_bytes=64),
-            sb.tile([P, C], F32, name="pv2", tag="w_then_pv2", align_bytes=64),
-        ]
-        for b in (pv[1], pv[0], pv[2]):
-            nc.gpsimd.memset(b[:], 0.0)
-        boards = [pw, [pv[t % 3] for t in range(PACK)]]
+        deal_scales(1, nc.gpsimd, 0, PACK)
 
         fmt = (E4M3, E5M2)
         place = (l_a, l_b)
-        acc = {}
+        banks = [psum.tile([P, J], F32, name="bank%d" % i) for i in range(4)]
+        bank_of = {(0, 0): 0, (1, 0): 0, (0, 2): 0, (0, 1): 1, (1, 1): 1, (0, 3): 1, (1, 2): 2, (1, 3): 3}
 
         def multiply(m, t):
-            bank = psum.tile([P, J], F32, name="bank")
             cols = slice(P * t, P * (t + 1))
             nc.tensor.matmul_mx(
-                out=bank[:], lhsT=w_codes[m][:, cols].bitcast(fmt[m]), lhsT_scale=w_plane[m][:, cols],
+                out=banks[bank_of[m, t]][:], lhsT=w_codes[m][:, cols].bitcast(fmt[m]), lhsT_scale=w_plane[m][:, cols],
                 rhs=xg_words[:].bitcast(E2M1), rhs_scale=xg_plane[:], start=True, stop=True,
             )
-            acc[m, t] = bank
 
         vals = {}
 
         def evacuate(m, t, on_vector):
-            v = sb.tile([P, J], F32, name="vals%d_%d" % (m, t))
+            name = "vals%d_%d" % (m, t)
+            vals[m, t] = sb.tile([P, J], F32, name=name, tag=name, align_bytes=64)
             if on_vector:
-                nc.vector.tensor_copy(out=v[:], in_=acc[m, t][:])
+                nc.vector.tensor_copy(out=vals[m, t][:], in_=banks[bank_of[m, t]][:])
             else:
-                nc.scalar.copy(out=v[:], in_=acc[m, t][:])
-            vals[m, t] = v
+                nc.scalar.copy(out=vals[m, t][:], in_=banks[bank_of[m, t]][:])
 
         def scatter(m, t, on_vector):
-            window = boards[m][t][:].indirect(place[m][:])
+            window = boards[m, t][:].indirect(place[m][:])
             if on_vector:
                 nc.vector.tensor_copy(window, vals[m, t][:])
             else:
                 nc.scalar.activation(window, vals[m, t][:], COPY)
 
         hid = sb.tile([P, O, PACK], BF16, align_bytes=64)
+        pg = [sb.tile([P, C], F32, name="pg%d" % t) for t in range(PACK - 1)]
+        pg.append(pg[-1])
 
-        def read_board(t):
-            pg = sb.tile([P, C], F32, name="pg%d" % t)
-            nc.vector.tensor_tensor(out=pg[:], in0=boards[0][t][:], in1=boards[1][t][:], op=ADD)
-            nc.vector.tensor_copy(hid[:, :, t], pg[:].indirect(l_read[:]))
+        def join(t, engine):
+            engine.tensor_tensor(out=pg[t][:], in0=boards[0, t][:], in1=boards[1, t][:], op=ADD)
 
-        for t in range(PACK):
-            multiply(0, t)
+        def read_board(t, o0, o1):
+            nc.vector.tensor_copy(hid[:, o0:o1, t], pg[t][:].indirect(l_read[:, o0 // 16 : o1 // 16]))
+
+        multiply(0, 0)
+        multiply(0, 1)
         evacuate(0, 0, True)
         evacuate(0, 1, False)
         scatter(0, 0, True)
-        evacuate(0, 2, False)
-        evacuate(0, 3, False)
         scatter(0, 1, False)
-        for t in range(PACK):
-            multiply(1, t)
-        scatter(0, 2, True)
-        scatter(0, 3, False)
+        multiply(1, 0)
+        multiply(1, 1)
+        multiply(1, 2)
+        multiply(1, 3)
+        clear_board(1, 2, nc.gpsimd, "x_words")
+        clear_board(0, 2, nc.gpsimd, "w_raw0")
+        clear_board(0, 3, nc.gpsimd, "ws_raw1")
+        boards[1, 3] = boards[1, 0]
         evacuate(1, 0, True)
+        evacuate(1, 2, True)
         evacuate(1, 1, False)
-        evacuate(1, 2, False)
+        evacuate(1, 3, False)
+        multiply(0, 2)
+        multiply(0, 3)
         scatter(1, 0, True)
         scatter(1, 1, False)
-        evacuate(1, 3, False)
-        read_board(0)
+        join(0, nc.gpsimd)
+        join(1, nc.gpsimd)
+        evacuate(0, 2, True)
+        evacuate(0, 3, True)
         scatter(1, 2, False)
-        read_board(1)
+        scatter(0, 2, True)
+        join(2, nc.gpsimd)
+        scatter(0, 3, False)
+        read_board(0, 0, O)
+        read_board(1, 0, O)
+        read_board(2, 0, O)
         scatter(1, 3, False)
-        read_board(2)
-        read_board(3)
+        join(3, nc.vector)
 
+        halves = [slice(0, O // 2), slice(O // 2, O)]
         hid_codes = sb.tile([P, O], U32, align_bytes=64)
         hid_plane = sb.tile([P, O], U8, align_bytes=64)
-        nc.vector.quantize_mx(out=hid_codes[:].bitcast(E5M2), scales=hid_plane[:], in_=hid[:].rearrange("p o t -> p (o t)"))
-
-        for h in range(N // P):
-            bank = psum.tile([P, O], F32, name="bank")
-            nc.tensor.matmul_mx(
-                out=bank[:], lhsT=wb_codes[:, 2 * P * h : 2 * P * (h + 1)].bitcast(E2M1), lhsT_scale=wb_plane[:, P * h : P * (h + 1)],
-                rhs=hid_codes[:].bitcast(E5M2), rhs_scale=hid_plane[:], start=True, stop=True,
+        for half in halves:
+            read_board(3, half.start, half.stop)
+        for half in halves:
+            nc.vector.quantize_mx(
+                out=hid_codes[:, half].bitcast(E5M2), scales=hid_plane[:, half],
+                in_=hid[:, half, :].rearrange("p o t -> p (o t)"),
             )
-            prod = sb.tile([P, O], F32, name="prod%d" % h)
-            first = sb.tile([P, E], F32, name="first%d" % h)
-            second = sb.tile([P, E], F32, name="second%d" % h)
+
+        prod = [sb.tile([P, O], F32, name="prod%d" % h) for h in range(N // P)]
+        for i, half in enumerate(halves):
+            for h in (1, 0):
+                bank = psum.tile([P, O // 2], F32, name="out_bank%d_%d" % (i, h))
+                nc.tensor.matmul_mx(
+                    out=bank[:], lhsT=wb_codes[:, 2 * P * h : 2 * P * (h + 1)].bitcast(E2M1), lhsT_scale=wb_plane[:, P * h : P * (h + 1)],
+                    rhs=hid_codes[:, half].bitcast(E5M2), rhs_scale=hid_plane[:, half], start=True, stop=True,
+                )
+                if h == 0:
+                    nc.vector.tensor_copy(out=prod[h][:, half], in_=bank[:])
+                else:
+                    nc.scalar.copy(out=prod[h][:, half], in_=bank[:])
+        picks = {}
+        for h in (1, 0):
+            for i, pair_list in enumerate((l_p1, l_p2)):
+                picks[h, i] = sb.tile([P, E], F32, name="pick%d_%d" % (h, i))
+                if h == 0:
+                    nc.vector.tensor_copy(picks[h, i][:], prod[h][:].indirect(pair_list[:]))
+                else:
+                    nc.scalar.activation(picks[h, i][:], prod[h][:].indirect(pair_list[:]), COPY)
+        for h, queue in ((1, nc.scalar), (0, nc.sync)):
             best = sb.tile([P, E], F32, name="best%d" % h)
-            if h == 0:
-                nc.vector.tensor_copy(out=prod[:], in_=bank[:])
-                nc.vector.tensor_copy(first[:], prod[:].indirect(l_p1[:]))
-                nc.vector.tensor_copy(second[:], prod[:].indirect(l_p2[:]))
-            else:
-                nc.scalar.copy(out=prod[:], in_=bank[:])
-                nc.scalar.activation(first[:], prod[:].indirect(l_p1[:]), COPY)
-                nc.scalar.activation(second[:], prod[:].indirect(l_p2[:]), COPY)
-            nc.vector.tensor_tensor(out=best[:], in0=first[:], in1=second[:], op=MAX)
-            nc.sync.dma_start(out=out[P * h : P * (h + 1), :], in_=best[:])
+            nc.vector.tensor_tensor(out=best[:], in0=picks[h, 0][:], in1=picks[h, 1][:], op=MAX)
+            queue.dma_start(out=out[P * h : P * (h + 1), :], in_=best[:])

@@ -46,21 +46,21 @@ def tile_list_twow_shared_one_bestoftwo_kernel(
         wb_codes = sb.tile([P, 2 * N], U8, align_bytes=64)
         wb_plane = sb.tile([P, N], U8, align_bytes=64)
 
-        nc.vector.memset(x_plane[:].bitcast(I32), 0)
+        nc.vector.memset(x_plane[:, : T // 2].bitcast(I32), 0)
+        nc.gpsimd.memset(x_plane[:, T // 2 :].bitcast(I32), 0)
         nc.vector.memset(ws_raw[0][:].bitcast(I32), 0)
         nc.gpsimd.memset(ws_raw[1][:].bitcast(I32), 0)
-        load_scale_rows(nc.gpsimd, ws_raw[1], w2_scales, (3,))
         nc.gpsimd.memset(wb_plane[:].bitcast(I32), 0)
 
         nc.sync.dma_start(l_tok[:], offs)
+        nc.sync.dma_start(l_a[:], offs2)
         load_scale_rows(nc.sync, x_plane, xt_scales, (0, 1))
         nc.sync.dma_start(out=x_words[:].bitcast(I32), in_=xt_words[0].bitcast(I32))
         load_scale_rows(nc.sync, x_plane, xt_scales, (2, 3))
         nc.sync.dma_start(out=w_raw[0][:].bitcast(I32), in_=w_words[0].rearrange("p n t -> p (n t)").bitcast(I32))
         load_scale_rows(nc.sync, ws_raw[0], w_scales, range(4))
         nc.sync.dma_start(out=w_raw[1][:].bitcast(I32), in_=w2_words[0].rearrange("p n t -> p (n t)").bitcast(I32))
-        nc.sync.dma_start(l_a[:], offs2)
-        load_scale_rows(nc.sync, ws_raw[1], w2_scales, range(3))
+        load_scale_rows(nc.sync, ws_raw[1], w2_scales, range(4))
         nc.sync.dma_start(l_b[:], offs3)
         nc.sync.dma_start(l_read[:], offs4)
         nc.sync.dma_start(out=wb_codes[:].bitcast(I32), in_=wb_words[0].bitcast(I32))
@@ -74,9 +74,8 @@ def tile_list_twow_shared_one_bestoftwo_kernel(
             boards[m, t] = sb.tile([P, C], F32, name="board%d_%d" % (m, t), tag=tag, align_bytes=64)
             engine.memset(boards[m, t][:], 0.0)
 
-        for m in range(2):
-            for t in range(2):
-                clear_board(m, t, nc.vector, "board%d_%d" % (m, t))
+        for t in range(PACK):
+            clear_board(0, t, nc.vector, "board0_%d" % t)
 
         xg_words = sb.tile([P, J], U16, align_bytes=64)
         xg_plane = sb.tile([P, J], U8, align_bytes=64)
@@ -102,12 +101,11 @@ def tile_list_twow_shared_one_bestoftwo_kernel(
         deal_scales(0, nc.vector, 0, 2)
         deal_scales(0, nc.vector, 2, PACK)
         deal_words(1)
-        deal_scales(1, nc.gpsimd, 0, PACK)
 
         fmt = (E4M3, E5M2)
         place = (l_a, l_b)
-        banks = [psum.tile([P, J], F32, name="bank%d" % i) for i in range(4)]
-        bank_of = {(0, 0): 0, (1, 0): 0, (0, 2): 0, (0, 1): 1, (1, 1): 1, (0, 3): 1, (1, 2): 2, (1, 3): 3}
+        banks = [psum.tile([P, J], F32, name="bank%d" % i) for i in range(6)]
+        bank_of = {(0, 0): 0, (0, 1): 1, (0, 2): 2, (0, 3): 3, (1, 0): 0, (1, 1): 1, (1, 2): 4, (1, 3): 5}
 
         def multiply(m, t):
             cols = slice(P * t, P * (t + 1))
@@ -118,9 +116,9 @@ def tile_list_twow_shared_one_bestoftwo_kernel(
 
         vals = {}
 
-        def evacuate(m, t, on_vector):
+        def evacuate(m, t, on_vector, tag=None):
             name = "vals%d_%d" % (m, t)
-            vals[m, t] = sb.tile([P, J], F32, name=name, tag=name, align_bytes=64)
+            vals[m, t] = sb.tile([P, J], F32, name=name, tag=tag or name, align_bytes=64)
             if on_vector:
                 nc.vector.tensor_copy(out=vals[m, t][:], in_=banks[bank_of[m, t]][:])
             else:
@@ -134,8 +132,7 @@ def tile_list_twow_shared_one_bestoftwo_kernel(
                 nc.scalar.activation(window, vals[m, t][:], COPY)
 
         hid = sb.tile([P, O, PACK], BF16, align_bytes=64)
-        pg = [sb.tile([P, C], F32, name="pg%d" % t) for t in range(PACK - 1)]
-        pg.append(pg[-1])
+        pg = [sb.tile([P, C], F32, name="pg%d" % t) for t in range(2)] * 2
 
         def join(t, engine):
             engine.tensor_tensor(out=pg[t][:], in0=boards[0, t][:], in1=boards[1, t][:], op=ADD)
@@ -143,47 +140,44 @@ def tile_list_twow_shared_one_bestoftwo_kernel(
         def read_board(t, o0, o1):
             nc.vector.tensor_copy(hid[:, o0:o1, t], pg[t][:].indirect(l_read[:, o0 // 16 : o1 // 16]))
 
-        multiply(0, 0)
-        multiply(0, 1)
+        for t in (0, 1, 3, 2):
+            multiply(0, t)
         evacuate(0, 0, True)
         evacuate(0, 1, False)
+        evacuate(0, 3, False)
         scatter(0, 0, True)
         scatter(0, 1, False)
-        multiply(1, 0)
-        multiply(1, 1)
-        multiply(1, 2)
-        multiply(1, 3)
-        clear_board(1, 2, nc.gpsimd, "x_words")
-        clear_board(0, 2, nc.gpsimd, "w_raw0")
-        clear_board(0, 3, nc.gpsimd, "ws_raw1")
-        boards[1, 3] = boards[1, 0]
-        evacuate(1, 0, True)
-        evacuate(1, 2, True)
+        clear_board(1, 1, nc.gpsimd, "w_raw1")
+        clear_board(1, 0, nc.gpsimd, "ws_raw0")
+        deal_scales(1, nc.vector, 0, PACK)
+        for t in range(PACK):
+            multiply(1, t)
+        evacuate(0, 2, True, "ws_raw1")
+        scatter(0, 2, True)
+        scatter(0, 3, False)
+        clear_board(1, 2, nc.gpsimd, "vals0_3")
+        boards[1, 3] = boards[1, 1]
+        evacuate(1, 0, False)
         evacuate(1, 1, False)
-        evacuate(1, 3, False)
-        multiply(0, 2)
-        multiply(0, 3)
+        evacuate(1, 2, False)
         scatter(1, 0, True)
         scatter(1, 1, False)
-        join(0, nc.gpsimd)
-        join(1, nc.gpsimd)
-        evacuate(0, 2, True)
-        evacuate(0, 3, True)
+        evacuate(1, 3, False)
         scatter(1, 2, False)
-        scatter(0, 2, True)
-        join(2, nc.gpsimd)
-        scatter(0, 3, False)
-        read_board(0, 0, O)
+        join(1, nc.vector)
+        join(0, nc.vector)
         read_board(1, 0, O)
-        read_board(2, 0, O)
+        read_board(0, 0, O)
         scatter(1, 3, False)
+        join(2, nc.vector)
+        read_board(2, 0, O)
         join(3, nc.vector)
-
-        halves = [slice(0, O // 2), slice(O // 2, O)]
-        hid_codes = sb.tile([P, O], U32, align_bytes=64)
-        hid_plane = sb.tile([P, O], U8, align_bytes=64)
+        halves = (slice(0, O // 2), slice(O // 2, O))
         for half in halves:
             read_board(3, half.start, half.stop)
+
+        hid_codes = sb.tile([P, O], U32, align_bytes=64)
+        hid_plane = sb.tile([P, O], U8, align_bytes=64)
         for half in halves:
             nc.vector.quantize_mx(
                 out=hid_codes[:, half].bitcast(E5M2), scales=hid_plane[:, half],
@@ -191,22 +185,21 @@ def tile_list_twow_shared_one_bestoftwo_kernel(
             )
 
         prod = [sb.tile([P, O], F32, name="prod%d" % h) for h in range(N // P)]
-        for i, half in enumerate(halves):
-            for h in (1, 0):
-                bank = psum.tile([P, O // 2], F32, name="out_bank%d_%d" % (i, h))
-                nc.tensor.matmul_mx(
-                    out=bank[:], lhsT=wb_codes[:, 2 * P * h : 2 * P * (h + 1)].bitcast(E2M1), lhsT_scale=wb_plane[:, P * h : P * (h + 1)],
-                    rhs=hid_codes[:, half].bitcast(E5M2), rhs_scale=hid_plane[:, half], start=True, stop=True,
-                )
-                if h == 0:
-                    nc.vector.tensor_copy(out=prod[h][:, half], in_=bank[:])
-                else:
-                    nc.scalar.copy(out=prod[h][:, half], in_=bank[:])
+        for h in (1, 0):
+            bank = psum.tile([P, O], F32, name="out_bank%d" % h)
+            nc.tensor.matmul_mx(
+                out=bank[:], lhsT=wb_codes[:, 2 * P * h : 2 * P * (h + 1)].bitcast(E2M1), lhsT_scale=wb_plane[:, P * h : P * (h + 1)],
+                rhs=hid_codes[:].bitcast(E5M2), rhs_scale=hid_plane[:], start=True, stop=True,
+            )
+            if h == 0:
+                nc.vector.tensor_copy(out=prod[h][:], in_=bank[:])
+            else:
+                nc.scalar.copy(out=prod[h][:], in_=bank[:])
         picks = {}
         for h in (1, 0):
             for i, pair_list in enumerate((l_p1, l_p2)):
                 picks[h, i] = sb.tile([P, E], F32, name="pick%d_%d" % (h, i))
-                if h == 0:
+                if i == 0:
                     nc.vector.tensor_copy(picks[h, i][:], prod[h][:].indirect(pair_list[:]))
                 else:
                     nc.scalar.activation(picks[h, i][:], prod[h][:].indirect(pair_list[:]), COPY)

@@ -46,20 +46,16 @@ def tile_list_twow_shared_one_bestoftwo_kernel(
         wb_codes = sb.tile([P, 2 * N], U8, align_bytes=64)
         wb_plane = sb.tile([P, N], U8, align_bytes=64)
 
-        nc.vector.memset(x_plane[:, : T // 2].bitcast(I32), 0)
-        nc.gpsimd.memset(x_plane[:, T // 2 :].bitcast(I32), 0)
-        nc.vector.memset(ws_raw[0][:].bitcast(I32), 0)
-        nc.gpsimd.memset(ws_raw[1][:].bitcast(I32), 0)
-        nc.gpsimd.memset(wb_plane[:].bitcast(I32), 0)
+        for plane in (x_plane, ws_raw[0], ws_raw[1], wb_plane):
+            nc.vector.memset(plane[:].bitcast(I32), 0)
 
-        nc.sync.dma_start(l_tok[:], offs)
-        nc.sync.dma_start(l_a[:], offs2)
-        load_scale_rows(nc.sync, x_plane, xt_scales, (0, 1))
         nc.sync.dma_start(out=x_words[:].bitcast(I32), in_=xt_words[0].bitcast(I32))
-        load_scale_rows(nc.sync, x_plane, xt_scales, (2, 3))
+        nc.sync.dma_start(l_tok[:], offs)
+        load_scale_rows(nc.sync, x_plane, xt_scales, range(4))
         nc.sync.dma_start(out=w_raw[0][:].bitcast(I32), in_=w_words[0].rearrange("p n t -> p (n t)").bitcast(I32))
         load_scale_rows(nc.sync, ws_raw[0], w_scales, range(4))
         nc.sync.dma_start(out=w_raw[1][:].bitcast(I32), in_=w2_words[0].rearrange("p n t -> p (n t)").bitcast(I32))
+        nc.sync.dma_start(l_a[:], offs2)
         load_scale_rows(nc.sync, ws_raw[1], w2_scales, range(4))
         nc.sync.dma_start(l_b[:], offs3)
         nc.sync.dma_start(l_read[:], offs4)
@@ -72,10 +68,13 @@ def tile_list_twow_shared_one_bestoftwo_kernel(
 
         def clear_board(m, t, engine, tag):
             boards[m, t] = sb.tile([P, C], F32, name="board%d_%d" % (m, t), tag=tag, align_bytes=64)
-            engine.memset(boards[m, t][:], 0.0)
+            engine.memset(boards[m, t][:].bitcast(I32), 0)
 
-        for t in range(PACK):
+        for t in range(PACK - 1):
             clear_board(0, t, nc.vector, "board0_%d" % t)
+        boards[0, 3] = boards[0, 0]
+        for t in range(PACK):
+            clear_board(1, t, nc.vector, "board1_%d" % t)
 
         xg_words = sb.tile([P, J], U16, align_bytes=64)
         xg_plane = sb.tile([P, J], U8, align_bytes=64)
@@ -131,54 +130,58 @@ def tile_list_twow_shared_one_bestoftwo_kernel(
             else:
                 nc.scalar.activation(window, vals[m, t][:], COPY)
 
+        rows = sb.tile([P, PACK, O], BF16, align_bytes=64)
         hid = sb.tile([P, O, PACK], BF16, align_bytes=64)
-        pg = [sb.tile([P, C], F32, name="pg%d" % t) for t in range(2)] * 2
+        pg = [sb.tile([P, C], F32, name="pg%d" % t) for t in range(PACK)]
 
-        def join(t, engine):
-            engine.tensor_tensor(out=pg[t][:], in0=boards[0, t][:], in1=boards[1, t][:], op=ADD)
+        def join(t):
+            nc.vector.tensor_tensor(out=pg[t][:], in0=boards[0, t][:], in1=boards[1, t][:], op=ADD)
 
-        def read_board(t, o0, o1):
-            nc.vector.tensor_copy(hid[:, o0:o1, t], pg[t][:].indirect(l_read[:, o0 // 16 : o1 // 16]))
+        def read_board(t, cols, on_vector):
+            window = pg[t][:].indirect(l_read[:, cols.start // 16 : cols.stop // 16])
+            if on_vector:
+                nc.vector.tensor_copy(rows[:, t, cols], window)
+            else:
+                nc.scalar.activation(rows[:, t, cols], window, COPY)
 
-        for t in (0, 1, 3, 2):
+        for t in range(PACK):
             multiply(0, t)
         evacuate(0, 0, True)
         evacuate(0, 1, False)
-        evacuate(0, 3, False)
+        evacuate(0, 2, False)
         scatter(0, 0, True)
         scatter(0, 1, False)
-        clear_board(1, 1, nc.gpsimd, "w_raw1")
-        clear_board(1, 0, nc.gpsimd, "ws_raw0")
         deal_scales(1, nc.vector, 0, PACK)
         for t in range(PACK):
             multiply(1, t)
-        evacuate(0, 2, True, "ws_raw1")
-        scatter(0, 2, True)
-        scatter(0, 3, False)
-        clear_board(1, 2, nc.gpsimd, "vals0_3")
-        boards[1, 3] = boards[1, 1]
-        evacuate(1, 0, False)
-        evacuate(1, 1, False)
-        evacuate(1, 2, False)
+        evacuate(0, 3, True, "ws_raw1")
+        evacuate(1, 0, True)
+        scatter(0, 2, False)
         scatter(1, 0, True)
-        scatter(1, 1, False)
-        evacuate(1, 3, False)
+        for t in (1, 2, 3):
+            evacuate(1, t, False)
+        scatter(1, 1, True)
         scatter(1, 2, False)
-        join(1, nc.vector)
-        join(0, nc.vector)
-        read_board(1, 0, O)
-        read_board(0, 0, O)
+        join(0)
+        join(1)
         scatter(1, 3, False)
-        join(2, nc.vector)
-        read_board(2, 0, O)
-        join(3, nc.vector)
+        scatter(0, 3, True)
+        join(2)
+        join(3)
+        for t in range(PACK - 1):
+            read_board(t, slice(0, O), False)
         halves = (slice(0, O // 2), slice(O // 2, O))
-        for half in halves:
-            read_board(3, half.start, half.stop)
+        read_board(3, halves[0], True)
+        read_board(3, halves[1], False)
 
         hid_codes = sb.tile([P, O], U32, align_bytes=64)
         hid_plane = sb.tile([P, O], U8, align_bytes=64)
-        for half in halves:
+        for half in reversed(halves):
+            nc.vector.tensor_copy(
+                out=hid[:, half, :].rearrange("p (c i) t -> p c t i", i=4),
+                in_=rows[:, :, half].rearrange("p t (c i) -> p c t i", i=4),
+            )
+        for half in reversed(halves):
             nc.vector.quantize_mx(
                 out=hid_codes[:, half].bitcast(E5M2), scales=hid_plane[:, half],
                 in_=hid[:, half, :].rearrange("p o t -> p (o t)"),
@@ -203,7 +206,7 @@ def tile_list_twow_shared_one_bestoftwo_kernel(
                     nc.vector.tensor_copy(picks[h, i][:], prod[h][:].indirect(pair_list[:]))
                 else:
                     nc.scalar.activation(picks[h, i][:], prod[h][:].indirect(pair_list[:]), COPY)
-        for h, queue in ((1, nc.scalar), (0, nc.sync)):
+        for h, queue in ((1, nc.sync), (0, nc.sync)):
             best = sb.tile([P, E], F32, name="best%d" % h)
             nc.vector.tensor_tensor(out=best[:], in0=picks[h, 0][:], in1=picks[h, 1][:], op=MAX)
             queue.dma_start(out=out[P * h : P * (h + 1), :], in_=best[:])

from contextlib import ExitStack

import concourse.mybir as mybir

K, T, J, R, C, O, N, E = 512, 1024, 256, 512, 512, 256, 256, 128
FLOPS = 2 * K * R * J * 2 + 2 * R * N * O

F32 = mybir.dt.float32
BF16 = mybir.dt.bfloat16
I32 = mybir.dt.int32
U32 = mybir.dt.uint32
U16 = mybir.dt.uint16
U8 = mybir.dt.uint8
E4M3 = mybir.dt.float8_e4m3fn_x4
E5M2 = mybir.dt.float8_e5m2_x4
E2M1 = mybir.dt.float4_e2m1fn_x4
COPY = mybir.ActivationFunctionType.Copy
ADD = mybir.AluOpType.add
MAX = mybir.AluOpType.max

P = 128
PACK = 4


def load_scale_rows(queue, plane, scales, quadrants):
    for q in quadrants:
        queue.dma_start(out=plane[32 * q : 32 * q + 4, :].bitcast(I32), in_=scales[0, 4 * q : 4 * q + 4, :].bitcast(I32))


def tile_list_twow_shared_one_bestoftwo_kernel(
    tc, xt_words, xt_scales, w_words, w_scales, w2_words, w2_scales, wb_words, wb_scales,
    offs, offs2, offs3, offs4, offs5, offs6, out,
):
    nc = tc.nc
    with ExitStack() as ctx:
        sb = ctx.enter_context(tc.tile_pool(name="sb", bufs=1))
        psum = ctx.enter_context(tc.psum_pool(name="psum", bufs=1))

        lists = [sb.tile([P, src.shape[1]], U16, name="list%d" % i) for i, src in enumerate((offs, offs2, offs3, offs4, offs5, offs6))]
        l_tok, l_a, l_b, l_read, l_p1, l_p2 = lists

        x_words = sb.tile([P, T], U16, tag="x_words", align_bytes=64)
        x_plane = sb.tile([P, T], U8, align_bytes=64)
        w_raw = [sb.tile([P, R], U32, name="w_raw%d" % m, tag="w_raw%d" % m, align_bytes=64) for m in range(2)]
        ws_raw = [sb.tile([P, R], U8, name="ws_raw%d" % m, tag="ws_raw%d" % m, align_bytes=64) for m in range(2)]
        wb_codes = sb.tile([P, 2 * N], U8, align_bytes=64)
        wb_plane = sb.tile([P, N], U8, align_bytes=64)

        for plane in (x_plane, ws_raw[0], ws_raw[1], wb_plane):
            nc.vector.memset(plane[:].bitcast(I32), 0)

        nc.sync.dma_start(out=x_words[:].bitcast(I32), in_=xt_words[0].bitcast(I32))
        nc.sync.dma_start(l_tok[:], offs)
        load_scale_rows(nc.sync, x_plane, xt_scales, range(4))
        nc.sync.dma_start(out=w_raw[0][:].bitcast(I32), in_=w_words[0].rearrange("p n t -> p (n t)").bitcast(I32))
        load_scale_rows(nc.sync, ws_raw[0], w_scales, range(4))
        nc.sync.dma_start(out=w_raw[1][:].bitcast(I32), in_=w2_words[0].rearrange("p n t -> p (n t)").bitcast(I32))
        nc.sync.dma_start(l_a[:], offs2)
        load_scale_rows(nc.sync, ws_raw[1], w2_scales, range(4))
        nc.sync.dma_start(l_b[:], offs3)
        nc.sync.dma_start(l_read[:], offs4)
        nc.sync.dma_start(out=wb_codes[:].bitcast(I32), in_=wb_words[0].bitcast(I32))
        load_scale_rows(nc.sync, wb_plane, wb_scales, range(4))
        nc.sync.dma_start(l_p1[:], offs5)
        nc.sync.dma_start(l_p2[:], offs6)

        boards = {}

        def clear_board(m, t, engine, tag):
            boards[m, t] = sb.tile([P, C], F32, name="board%d_%d" % (m, t), tag=tag, align_bytes=64)
            engine.memset(boards[m, t][:].bitcast(I32), 0)

        for t in range(PACK - 1):
            clear_board(0, t, nc.vector, "board0_%d" % t)
        boards[0, 3] = boards[0, 0]
        for t in range(PACK):
            clear_board(1, t, nc.vector, "board1_%d" % t)

        xg_words = sb.tile([P, J], U16, align_bytes=64)
        xg_plane = sb.tile([P, J], U8, align_bytes=64)
        nc.vector.tensor_copy(xg_words[:], x_words[:].indirect(l_tok[:]))
        nc.vector.tensor_copy(xg_plane[:], x_plane[:].indirect(l_tok[:]))

        w_codes = [sb.tile([P, R], U32, name="w_codes%d" % m, align_bytes=64) for m in range(2)]
        w_plane = [sb.tile([P, R], U8, name="w_plane%d" % m, align_bytes=64) for m in range(2)]

        def deal_words(m):
            nc.scalar.copy(
                out=w_codes[m][:].rearrange("p (t c i) -> p c t i", t=PACK, i=4),
                in_=w_raw[m][:].rearrange("p (c i t) -> p c t i", t=PACK, i=4),
            )

        def deal_scales(m, engine, t0, t1):
            engine.tensor_copy(
                out=w_plane[m][:].rearrange("p (t q) -> p t q", t=PACK)[:, t0:t1, :],
                in_=ws_raw[m][:].rearrange("p (q t) -> p t q", t=PACK)[:, t0:t1, :],
            )

        deal_words(0)
        deal_scales(0, nc.vector, 0, 2)
        deal_scales(0, nc.vector, 2, PACK)
        deal_words(1)

        fmt = (E4M3, E5M2)
        place = (l_a, l_b)
        banks = [psum.tile([P, J], F32, name="bank%d" % i) for i in range(6)]
        bank_of = {(0, 0): 0, (0, 1): 1, (0, 2): 2, (0, 3): 3, (1, 0): 0, (1, 1): 1, (1, 2): 4, (1, 3): 5}

        def multiply(m, t):
            cols = slice(P * t, P * (t + 1))
            nc.tensor.matmul_mx(
                out=banks[bank_of[m, t]][:], lhsT=w_codes[m][:, cols].bitcast(fmt[m]), lhsT_scale=w_plane[m][:, cols],
                rhs=xg_words[:].bitcast(E2M1), rhs_scale=xg_plane[:], start=True, stop=True,
            )

        vals = {}

        def evacuate(m, t, on_vector, tag=None):
            name = "vals%d_%d" % (m, t)
            vals[m, t] = sb.tile([P, J], F32, name=name, tag=tag or name, align_bytes=64)
            if on_vector:
                nc.vector.tensor_copy(out=vals[m, t][:], in_=banks[bank_of[m, t]][:])
            else:
                nc.scalar.copy(out=vals[m, t][:], in_=banks[bank_of[m, t]][:])

        def scatter(m, t, on_vector):
            window = boards[m, t][:].indirect(place[m][:])
            if on_vector:
                nc.vector.tensor_copy(window, vals[m, t][:])
            else:
                nc.scalar.activation(window, vals[m, t][:], COPY)

        rows = sb.tile([P, PACK, O], BF16, align_bytes=64)
        hid = sb.tile([P, O, PACK], BF16, align_bytes=64)
        pg = [sb.tile([P, C], F32, name="pg%d" % t) for t in range(PACK)]

        def join(t):
            nc.vector.tensor_tensor(out=pg[t][:], in0=boards[0, t][:], in1=boards[1, t][:], op=ADD)

        def read_board(t, cols, on_vector):
            window = pg[t][:].indirect(l_read[:, cols.start // 16 : cols.stop // 16])
            if on_vector:
                nc.vector.tensor_copy(rows[:, t, cols], window)
            else:
                nc.scalar.activation(rows[:, t, cols], window, COPY)

        for t in range(PACK):
            multiply(0, t)
        evacuate(0, 0, True)
        evacuate(0, 1, False)
        evacuate(0, 2, False)
        scatter(0, 0, True)
        scatter(0, 1, False)
        deal_scales(1, nc.vector, 0, PACK)
        for t in range(PACK):
            multiply(1, t)
        evacuate(0, 3, True, "ws_raw1")
        evacuate(1, 0, True)
        scatter(0, 2, False)
        scatter(1, 0, True)
        for t in (1, 2, 3):
            evacuate(1, t, False)
        scatter(1, 1, True)
        scatter(1, 2, False)
        join(0)
        join(1)
        scatter(1, 3, False)
        scatter(0, 3, True)
        join(2)
        join(3)
        for t in range(PACK - 1):
            read_board(t, slice(0, O), False)
        halves = (slice(0, O // 2), slice(O // 2, O))
        read_board(3, halves[0], True)
        read_board(3, halves[1], False)

        hid_codes = sb.tile([P, O], U32, align_bytes=64)
        hid_plane = sb.tile([P, O], U8, align_bytes=64)
        for half in reversed(halves):
            nc.vector.tensor_copy(
                out=hid[:, half, :].rearrange("p (c i) t -> p c t i", i=4),
                in_=rows[:, :, half].rearrange("p t (c i) -> p c t i", i=4),
            )
        for half in reversed(halves):
            nc.vector.quantize_mx(
                out=hid_codes[:, half].bitcast(E5M2), scales=hid_plane[:, half],
                in_=hid[:, half, :].rearrange("p o t -> p (o t)"),
            )

        prod = [sb.tile([P, O], F32, name="prod%d" % h) for h in range(N // P)]
        for h in (1, 0):
            bank = psum.tile([P, O], F32, name="out_bank%d" % h)
            nc.tensor.matmul_mx(
                out=bank[:], lhsT=wb_codes[:, 2 * P * h : 2 * P * (h + 1)].bitcast(E2M1), lhsT_scale=wb_plane[:, P * h : P * (h + 1)],
                rhs=hid_codes[:].bitcast(E5M2), rhs_scale=hid_plane[:], start=True, stop=True,
            )
            if h == 0:
                nc.vector.tensor_copy(out=prod[h][:], in_=bank[:])
            else:
                nc.scalar.copy(out=prod[h][:], in_=bank[:])
        picks = {}
        for h in (1, 0):
            for i, pair_list in enumerate((l_p1, l_p2)):
                picks[h, i] = sb.tile([P, E], F32, name="pick%d_%d" % (h, i))
                if i == 0:
                    nc.vector.tensor_copy(picks[h, i][:], prod[h][:].indirect(pair_list[:]))
                else:
                    nc.scalar.activation(picks[h, i][:], prod[h][:].indirect(pair_list[:]), COPY)
        for h, queue in ((1, nc.sync), (0, nc.sync)):
            best = sb.tile([P, E], F32, name="best%d" % h)
            nc.vector.tensor_tensor(out=best[:], in0=picks[h, 0][:], in1=picks[h, 1][:], op=MAX)
            queue.dma_start(out=out[P * h : P * (h + 1), :], in_=best[:])
